import numpy as np
import ml_dtypes


def mxq(x, axis, fmt="e4m3"):
    dtype, down = {"e4m3": (ml_dtypes.float8_e4m3fn, 7), "e5m2": (ml_dtypes.float8_e5m2, 14)}[fmt]
    v = np.moveaxis(np.asarray(x, np.float32).astype(ml_dtypes.bfloat16).astype(np.float64), axis, -1)
    blocks = v.reshape(v.shape[:-1] + (-1, 32))
    amax = np.abs(blocks).max(-1, keepdims=True)
    byte = np.maximum(np.where(amax > 0, np.frexp(amax)[1] - 1 + 127, 0) - down, 1)
    scale = np.exp2(byte - 127.0)
    codes = (blocks / scale).astype(np.float32).astype(dtype).astype(np.float64)
    return np.moveaxis((codes * scale).reshape(v.shape), -1, axis)


WIDE = False


def mx_kscale(k):
    if not WIDE:
        return np.ones(k)
    levels = np.array([24, -24, 12, -12, 0])
    if k % 512:
        return np.exp2(np.random.permutation(np.resize(levels, k // 32))).repeat(32)
    a = np.empty((k // 512, 16))
    for p in range(k // 512):
        a[p, :8] = np.random.permutation(np.resize(levels, 8))
        for g in range(8):
            far = levels[np.abs(levels - a[p, g]) >= 10]
            a[p, g + 8] = far[np.random.randint(len(far))]
    return np.exp2(a.ravel()).repeat(32)


def f64(x):
    return np.asarray(x).astype(np.float64)


def striped8(idx):
    return np.concatenate([v.reshape(-1, 16).T for v in idx]).astype(np.uint16)


def unstriped8(offs):
    return np.stack([offs[16 * g:16 * g + 16].T.reshape(-1) for g in range(8)]).astype(np.int64)


E2M1 = np.array([0.0, 0.5, 1.0, 1.5, 2.0, 3.0, 4.0, 6.0, -0.0, -0.5, -1.0, -1.5, -2.0, -3.0, -4.0, -6.0])


def pack_weight(w, fmt):
    k, n = w.shape
    w = f64(np.asarray(w, np.float32).astype(ml_dtypes.bfloat16)).reshape(k // 32, 32, n)
    amax = np.abs(w).max(1)
    if fmt == "e4m3":
        byte = np.frexp(amax)[1] - 1 + 127 - 7
    else:
        mant, ex = np.frexp(amax / 6.0)
        byte = np.where(mant > 0.5, ex, ex - 1) + 127
    byte = np.clip(np.where(amax > 0, byte, 1), 1, 254)
    scaled = (w * np.exp2(127.0 - byte)[:, None, :]).reshape(k, n).astype(np.float32)
    by_word = np.ascontiguousarray(scaled.reshape(k // 512, 128, 4, n).transpose(0, 1, 3, 2))
    if fmt == "e4m3":
        words = by_word.astype(ml_dtypes.float8_e4m3fn).view(np.uint8)
    else:
        c = by_word.astype(ml_dtypes.float4_e2m1fn).view(np.uint8) & 0xF
        words = (c[..., 0::2] | (c[..., 1::2] << 4)).reshape(k // 512, 128, 2 * n)
    return np.ascontiguousarray(words), np.ascontiguousarray(byte.astype(np.uint8).reshape(k // 512, 16, n))


def unpack_weight(words, scales, fmt):
    g, _, n = scales.shape
    words = np.ascontiguousarray(words).reshape(g, 128, n, -1)
    if fmt == "e4m3":
        vals = words.view(ml_dtypes.float8_e4m3fn).astype(np.float64)
    else:
        nib = np.empty((g, 128, n, 4), np.uint8)
        nib[..., 0::2] = words & 0xF
        nib[..., 1::2] = words >> 4
        vals = E2M1[nib]
    vals = vals * np.repeat(np.exp2(scales.astype(np.float64) - 127.0), 8, axis=1)[..., None]
    return vals.transpose(0, 1, 3, 2).reshape(g * 512, n)


K, L, N, T, J = 512, 512, 512, 2048, 1024


def setup_inputs():
    n = np.random.standard_normal
    s = mx_kscale(K)[:, None]
    s2 = mx_kscale(L)[:, None]
    p_wa = pack_weight(n((K, N)) / np.sqrt(K) / s, "e4m3")
    p_wb = pack_weight(n((L, N)) / np.sqrt(L) / s2, "e2m1")
    return {
        "xT": (n((K, T)) * s).astype(np.float32),
        "wgt": np.repeat(np.random.uniform(0.5, 2.0, (8, J)), 16, axis=0).astype(np.float32),
        "zT": (n((L, T)) * s2).astype(np.float32),
        "wgt2": np.repeat(np.random.uniform(0.5, 2.0, (8, J)), 16, axis=0).astype(np.float32),
        "wa_words": p_wa[0],
        "wa_scales": p_wa[1],
        "wb_words": p_wb[0],
        "wb_scales": p_wb[1],
        "offs": striped8(np.stack([np.random.permutation(T)[:J] for _ in range(8)])),
        "offs2": striped8(np.stack([np.random.permutation(T)[:J] for _ in range(8)])),
    }


def reference(xT, wgt, zT, wgt2, wa_words, wa_scales, wb_words, wb_scales, offs, offs2):
    idx = unstriped8(offs)
    idx2 = unstriped8(offs2)
    rows = np.arange(K)
    xg = f64(wgt)[rows // 4 % 128] * f64(xT)[rows[:, None], idx[rows % 512 // 64]]
    xT_ = mxq(xg, 0, "e4m3")
    rows = np.arange(L)
    xg = f64(wgt2)[rows // 4 % 128] * f64(zT)[rows[:, None], idx2[rows % 512 // 64]]
    zT_ = mxq(xg, 0, "e4m3")
    wa_ = unpack_weight(wa_words, wa_scales, "e4m3")
    wb_ = unpack_weight(wb_words, wb_scales, "e2m1")
    ya = wa_.T @ xT_
    yb = wb_.T @ zT_
    return np.maximum(ya, yb)

@@ -1,0 +1,160 @@
+from contextlib import ExitStack
+
+import concourse.mybir as mybir
+
+K, N, T, J = 512, 512, 2048, 1024
+FLOPS = 2 * 2 * K * N * J
+
+F32 = mybir.dt.float32
+BF16 = mybir.dt.bfloat16
+I32 = mybir.dt.int32
+U32 = mybir.dt.uint32
+U16 = mybir.dt.uint16
+U8 = mybir.dt.uint8
+FP8X4 = mybir.dt.float8_e4m3fn_x4
+FP4X4 = mybir.dt.float4_e2m1fn_x4
+MULT = mybir.AluOpType.mult
+MAX = mybir.AluOpType.max
+
+P = 128
+PACK = 4
+N_TILES = N // P
+BANK = 512
+HALF = 512
+QUARTER = 256
+
+
+def tile_list_max_none_kernel(
+    tc, xT, wgt, zT, wgt2, wa_words, wa_scales, wb_words, wb_scales, offs, offs2, out
+):
+    nc = tc.nc
+    with ExitStack() as ctx:
+        keep = ctx.enter_context(tc.tile_pool(name="keep", bufs=1))
+        psum = ctx.enter_context(tc.psum_pool(name="psum", bufs=8))
+
+        z_offsets = keep.tile([P, J // 16], U16, name="z_offsets")
+        x_offsets = keep.tile([P, J // 16], U16, name="x_offsets")
+        z_planes = [keep.tile([P, T], F32, name=f"z_plane{i}") for i in range(PACK)]
+        x_planes = [keep.tile([P, T], F32, name=f"x_plane{i}") for i in range(PACK)]
+        z_gain = [keep.tile([P, HALF], F32, name=f"z_gain{h}") for h in range(2)]
+        x_gain = keep.tile([P, J], F32, name="x_gain")
+        wa_codes = keep.tile([P, PACK * N], U8, name="wa_codes", align_bytes=64)
+        wb_codes = keep.tile([P, 2 * N], U8, name="wb_codes", align_bytes=64)
+        wa_exp = keep.tile([P, N], U8, name="wa_exp", align_bytes=64)
+        wb_exp = keep.tile([P, N], U8, name="wb_exp", align_bytes=64)
+
+        z_rows = zT.rearrange("(p i) t -> i p t", i=PACK)
+        x_rows = xT.rearrange("(p i) t -> i p t", i=PACK)
+
+        nc.vector.memset(wb_exp[:].bitcast(I32), 0)
+        nc.vector.memset(wa_exp[:].bitcast(I32), 0)
+
+        def load_scales(plane, scales):
+            for q in range(4):
+                nc.sync.dma_start(
+                    plane[32 * q : 32 * q + 4, :].bitcast(I32), scales[0, 4 * q : 4 * q + 4, :].bitcast(I32)
+                )
+
+        nc.sync.dma_start(z_offsets[:], offs2)
+        nc.sync.dma_start(z_planes[0][:], z_rows[0])
+        for h in range(2):
+            nc.sync.dma_start(z_gain[h][:], wgt2[:, h * HALF : (h + 1) * HALF])
+        for i in range(1, PACK):
+            nc.sync.dma_start(z_planes[i][:], z_rows[i])
+        nc.sync.dma_start(x_offsets[:], offs)
+        load_scales(wb_exp, wb_scales)
+        nc.sync.dma_start(x_planes[0][:], x_rows[0])
+        nc.sync.dma_start(x_gain[:], wgt)
+        nc.sync.dma_start(wb_codes[:].bitcast(I32), wb_words[0].bitcast(I32))
+        load_scales(wa_exp, wa_scales)
+        for i in range(1, PACK):
+            nc.sync.dma_start(x_planes[i][:], x_rows[i])
+        nc.sync.dma_start(wa_codes[:].bitcast(I32), wa_words[0].rearrange("p n i -> p (n i)").bitcast(I32))
+
+        def gather(picked, planes, i, offsets, gain, j0, width):
+            window = planes[i][:].indirect(offsets[:, j0 // 16 : (j0 + width) // 16])
+            nc.vector.tensor_tensor(picked[:, i, :], window, gain, MULT)
+
+        def interleave(picked, name):
+            width = picked.shape[2]
+            woven = keep.tile([P, width, PACK], BF16, name=name, align_bytes=64)
+            nc.scalar.copy(
+                woven[:].rearrange("p (c e) i -> p c i e", e=4),
+                picked[:].rearrange("p i (c e) -> p c i e", e=4),
+            )
+            return woven
+
+        def quantize(woven, name):
+            width = woven.shape[1]
+            codes = keep.tile([P, width], U32, name=name + "_codes", align_bytes=64)
+            exps = keep.tile([P, width], U8, name=name + "_exp", align_bytes=64)
+            nc.vector.quantize_mx(
+                out=codes[:].bitcast(FP8X4), scales=exps[:], in_=woven[:].rearrange("p j i -> p (j i)")
+            )
+            return codes, exps
+
+        z_picked = [keep.tile([P, PACK, HALF], F32, name=f"z_picked{h}") for h in range(2)]
+        for i in range(PACK):
+            for h in range(2):
+                gather(z_picked[h], z_planes, i, z_offsets, z_gain[h][:], h * HALF, HALF)
+        z_woven = [interleave(z_picked[h], f"z_woven{h}") for h in range(2)]
+
+        x_picked = [keep.tile([P, PACK, QUARTER], F32, name=f"x_picked{q}") for q in range(4)]
+
+        def gather_x(i):
+            for q in range(4):
+                gather(x_picked[q], x_planes, i, x_offsets, x_gain[:, q * QUARTER : (q + 1) * QUARTER], q * QUARTER, QUARTER)
+
+        yb = [keep.tile([P, N_TILES, QUARTER], F32, name=f"yb{q}") for q in range(4)]
+        for h in range(2):
+            gather_x(h)
+            codes, exps = quantize(z_woven[h], f"z{h}")
+            for n in range(N_TILES):
+                bank = psum.tile([P, BANK], F32, name="bank")
+                nc.tensor.matmul_mx(
+                    out=bank[:],
+                    lhsT=wb_codes[:, 2 * P * n : 2 * P * (n + 1)].bitcast(FP4X4),
+                    lhsT_scale=wb_exp[:, P * n : P * (n + 1)],
+                    rhs=codes[:].bitcast(FP8X4),
+                    rhs_scale=exps[:],
+                    start=True,
+                    stop=True,
+                )
+                for u in range(2):
+                    nc.scalar.copy(yb[2 * h + u][:, n, :], bank[:, u * QUARTER : (u + 1) * QUARTER])
+        gather_x(2)
+        gather_x(3)
+        x_woven = [interleave(x_picked[q], f"x_woven{q}") for q in range(4)]
+
+        out_rows = out.rearrange("(n p) j -> p n j", p=P)
+
+        def multiply_x(q):
+            codes, exps = quantize(x_woven[q], f"x{q}")
+            banks = []
+            for pair in range(2):
+                bank = psum.tile([P, 2, QUARTER], F32, name="bank")
+                for u in range(2):
+                    n = 2 * pair + u
+                    nc.tensor.matmul_mx(
+                        out=bank[:, u, :],
+                        lhsT=wa_codes[:, PACK * P * n : PACK * P * (n + 1)].bitcast(FP8X4),
+                        lhsT_scale=wa_exp[:, P * n : P * (n + 1)],
+                        rhs=codes[:].bitcast(FP8X4),
+                        rhs_scale=exps[:],
+                        start=True,
+                        stop=True,
+                    )
+                banks.append(bank)
+            return banks
+
+        def finish(q, pair, bank):
+            result = keep.tile([P, 2, QUARTER], F32, name=f"result{q}_{pair}")
+            nc.vector.tensor_tensor(result[:], bank[:], yb[q][:, 2 * pair : 2 * pair + 2, :], MAX)
+            nc.sync.dma_start(out_rows[:, 2 * pair : 2 * pair + 2, q * QUARTER : (q + 1) * QUARTER], result[:])
+
+        banks = multiply_x(0)
+        for q in range(4):
+            finish(q, 0, banks[0])
+            following = multiply_x(q + 1) if q + 1 < 4 else None
+            finish(q, 1, banks[1])
+            banks = following

@@ -1,6 +1,7 @@
 from contextlib import ExitStack
 
 import concourse.mybir as mybir
+from concourse.masks import make_identity
 
 K, N, T, J = 512, 512, 2048, 1024
 FLOPS = 2 * 2 * K * N * J
@@ -18,6 +19,10 @@ MAX = mybir.AluOpType.max
 
 P = 128
 PACK = 4
+GROUPS = 8
+GROUP_ROWS = P // GROUPS
+CHUNKS = J // P
+REPEAT = 8
 N_TILES = N // P
 BANK = 512
 HALF = 512
@@ -35,19 +40,31 @@ def tile_list_max_none_kernel(
         z_offsets = keep.tile([P, J // 16], U16, name="z_offsets")
         x_offsets = keep.tile([P, J // 16], U16, name="x_offsets")
         z_planes = [keep.tile([P, T], F32, name=f"z_plane{i}") for i in range(PACK)]
-        x_planes = [keep.tile([P, T], F32, name=f"x_plane{i}") for i in range(PACK)]
-        z_gain = [keep.tile([P, HALF], F32, name=f"z_gain{h}") for h in range(2)]
-        x_gain = keep.tile([P, J], F32, name="x_gain")
+        x_planes = [keep.tile([P, T], F32, name=f"x_plane{i}", align_bytes=64) for i in range(PACK)]
+        z_picked = [keep.tile([P, PACK * HALF], F32, name=f"z_picked{h}") for h in range(2)]
+        x_picked = [
+            keep.tile([P, PACK * HALF], F32, name=f"x_picked{h}", align_bytes=64) for h in range(2)
+        ]
+        z_gain = [keep.tile([P, HALF], F32, name=f"z_gain{h}", align_bytes=64)[:] for h in range(2)]
+        x_gain1 = keep.tile([P, HALF], F32, name="x_gain1")
+        x_gain = [x_picked[1][:, 2 * HALF + QUARTER : 3 * HALF + QUARTER], x_gain1[:]]
         wa_codes = keep.tile([P, PACK * N], U8, name="wa_codes", align_bytes=64)
         wb_codes = keep.tile([P, 2 * N], U8, name="wb_codes", align_bytes=64)
         wa_exp = keep.tile([P, N], U8, name="wa_exp", align_bytes=64)
         wb_exp = keep.tile([P, N], U8, name="wb_exp", align_bytes=64)
+        z_compact = keep.tile([P, P], F32, name="z_compact", align_bytes=64)
+        x_compact = keep.tile([P, P], F32, name="x_compact")
+        identity = keep.tile([P, P], F32, name="identity")
 
         z_rows = zT.rearrange("(p i) t -> i p t", i=PACK)
         x_rows = xT.rearrange("(p i) t -> i p t", i=PACK)
 
+        make_identity(nc, identity[:])
         nc.vector.memset(wb_exp[:].bitcast(I32), 0)
         nc.vector.memset(wa_exp[:].bitcast(I32), 0)
+
+        def load_compact(compact, gains):
+            nc.sync.dma_start(compact[:], gains[0:P:REPEAT, :].rearrange("m (c j) -> m c j", j=P))
 
         def load_scales(plane, scales):
             for q in range(4):
@@ -55,81 +72,110 @@ def tile_list_max_none_kernel(
                     plane[32 * q : 32 * q + 4, :].bitcast(I32), scales[0, 4 * q : 4 * q + 4, :].bitcast(I32)
                 )
 
+        load_compact(z_compact, wgt2)
         nc.sync.dma_start(z_offsets[:], offs2)
         nc.sync.dma_start(z_planes[0][:], z_rows[0])
-        for h in range(2):
-            nc.sync.dma_start(z_gain[h][:], wgt2[:, h * HALF : (h + 1) * HALF])
+        load_compact(x_compact, wgt)
         for i in range(1, PACK):
             nc.sync.dma_start(z_planes[i][:], z_rows[i])
         nc.sync.dma_start(x_offsets[:], offs)
         load_scales(wb_exp, wb_scales)
         nc.sync.dma_start(x_planes[0][:], x_rows[0])
-        nc.sync.dma_start(x_gain[:], wgt)
         nc.sync.dma_start(wb_codes[:].bitcast(I32), wb_words[0].bitcast(I32))
         load_scales(wa_exp, wa_scales)
         for i in range(1, PACK):
             nc.sync.dma_start(x_planes[i][:], x_rows[i])
         nc.sync.dma_start(wa_codes[:].bitcast(I32), wa_words[0].rearrange("p n i -> p (n i)").bitcast(I32))
 
-        def gather(picked, planes, i, offsets, gain, j0, width):
-            window = planes[i][:].indirect(offsets[:, j0 // 16 : (j0 + width) // 16])
-            nc.vector.tensor_tensor(picked[:, i, :], window, gain, MULT)
+        chunks = HALF // P
+        z_turned = keep.tile([P, P], F32, name="z_turned", align_bytes=64)
+        nc.vector.transpose(z_turned[:], z_compact[:])
+        z_repeated = [keep.tile([P, HALF], F32, name=f"z_repeated{h}", align_bytes=64) for h in range(2)]
+        for h in range(2):
+            source = z_turned[:].rearrange("p (b m c) -> p c b m", b=4, m=4)[:, h * chunks : (h + 1) * chunks]
+            nc.vector.tensor_copy(
+                z_repeated[h][:].rearrange("p (c b m r) -> p c b m r", b=4, m=4, r=REPEAT),
+                source.unsqueeze(4).to_broadcast([P, chunks, 4, 4, REPEAT]),
+            )
+        for h in range(2):
+            nc.vector.transpose(z_gain[h], z_repeated[h][:])
 
-        def interleave(picked, name):
-            width = picked.shape[2]
-            woven = keep.tile([P, width, PACK], BF16, name=name, align_bytes=64)
+        x_turned = psum.tile([P, P], F32, name="bank")
+        nc.tensor.transpose(x_turned[:], x_compact[:], identity[:])
+        for h in range(2):
+            source = x_turned[:].rearrange("p (m c) -> p c m", c=CHUNKS)[:, h * chunks : (h + 1) * chunks]
+            repeated = keep.tile([P, HALF], F32, name=f"x_repeated{h}")
             nc.scalar.copy(
-                woven[:].rearrange("p (c e) i -> p c i e", e=4),
-                picked[:].rearrange("p i (c e) -> p c i e", e=4),
+                repeated[:].rearrange("p (c m r) -> p c m r", c=chunks, r=REPEAT),
+                source.unsqueeze(3).to_broadcast([P, chunks, P // REPEAT, REPEAT]),
             )
-            return woven
+            bank = psum.tile([P, BANK], F32, name="bank")
+            for c in range(chunks):
+                nc.tensor.transpose(bank[:, c * P : (c + 1) * P], repeated[:, c * P : (c + 1) * P], identity[:])
+            nc.scalar.copy(x_gain[h], bank[:])
 
-        def quantize(woven, name):
-            width = woven.shape[1]
-            codes = keep.tile([P, width], U32, name=name + "_codes", align_bytes=64)
-            exps = keep.tile([P, width], U8, name=name + "_exp", align_bytes=64)
-            nc.vector.quantize_mx(
-                out=codes[:].bitcast(FP8X4), scales=exps[:], in_=woven[:].rearrange("p j i -> p (j i)")
+        def gather(picked, planes, offsets, gain, i, h, j0=0, width=HALF):
+            first = h * HALF + j0
+            window = planes[i][:].indirect(offsets[:, first // 16 : (first + width) // 16])
+            nc.vector.tensor_tensor(
+                picked[h][:, i * HALF + j0 : i * HALF + j0 + width], window, gain[h][:, j0 : j0 + width], MULT
             )
-            return codes, exps
 
-        z_picked = [keep.tile([P, PACK, HALF], F32, name=f"z_picked{h}") for h in range(2)]
+        def interleave(woven, picked, j0):
+            width = woven.shape[1] // PACK
+            planes = picked[:, : PACK * HALF].rearrange("p (i j) -> p i j", i=PACK)
+            nc.scalar.copy(
+                woven.rearrange("p (c e i) -> p c i e", e=4, i=PACK),
+                planes[:, :, j0 : j0 + width].rearrange("p i (c e) -> p c i e", e=4),
+            )
+
+        def quantize(woven, codes, name):
+            exps = keep.tile([P, codes.shape[1]], U8, name=name, align_bytes=64)
+            nc.vector.quantize_mx(out=codes.bitcast(FP8X4), scales=exps[:], in_=woven)
+            return exps
+
         for i in range(PACK):
             for h in range(2):
-                gather(z_picked[h], z_planes, i, z_offsets, z_gain[h][:], h * HALF, HALF)
-        z_woven = [interleave(z_picked[h], f"z_woven{h}") for h in range(2)]
-
-        x_picked = [keep.tile([P, PACK, QUARTER], F32, name=f"x_picked{q}") for q in range(4)]
-
-        def gather_x(i):
-            for q in range(4):
-                gather(x_picked[q], x_planes, i, x_offsets, x_gain[:, q * QUARTER : (q + 1) * QUARTER], q * QUARTER, QUARTER)
-
-        yb = [keep.tile([P, N_TILES, QUARTER], F32, name=f"yb{q}") for q in range(4)]
+                gather(z_picked, z_planes, z_offsets, z_gain, i, h)
+        z_woven = [keep.tile([P, PACK * HALF], BF16, name=f"z_woven{h}", align_bytes=64)[:] for h in range(2)]
         for h in range(2):
-            gather_x(h)
-            codes, exps = quantize(z_woven[h], f"z{h}")
+            interleave(z_woven[h], z_picked[h], 0)
+
+        yb = [keep.tile([P, N_TILES, HALF], F32, name=f"yb{h}") for h in range(2)]
+        for h in range(2):
+            gather(x_picked, x_planes, x_offsets, x_gain, 0, h)
+        z_codes = keep.tile([P, J], U32, name="z_codes", tag="x_plane0", align_bytes=64)
+        for h in range(2):
+            codes = z_codes[:, h * HALF : (h + 1) * HALF]
+            exps = quantize(z_woven[h], codes, f"z_exp{h}")
             for n in range(N_TILES):
                 bank = psum.tile([P, BANK], F32, name="bank")
                 nc.tensor.matmul_mx(
                     out=bank[:],
                     lhsT=wb_codes[:, 2 * P * n : 2 * P * (n + 1)].bitcast(FP4X4),
                     lhsT_scale=wb_exp[:, P * n : P * (n + 1)],
-                    rhs=codes[:].bitcast(FP8X4),
+                    rhs=codes.bitcast(FP8X4),
                     rhs_scale=exps[:],
                     start=True,
                     stop=True,
                 )
-                for u in range(2):
-                    nc.scalar.copy(yb[2 * h + u][:, n, :], bank[:, u * QUARTER : (u + 1) * QUARTER])
-        gather_x(2)
-        gather_x(3)
-        x_woven = [interleave(x_picked[q], f"x_woven{q}") for q in range(4)]
+                nc.scalar.copy(yb[h][:, n, :], bank[:])
+        for h in range(2):
+            gather(x_picked, x_planes, x_offsets, x_gain, 1, h)
+        gather(x_picked, x_planes, x_offsets, x_gain, 2, 0)
+        gather(x_picked, x_planes, x_offsets, x_gain, 3, 0, 0, QUARTER)
+        gather(x_picked, x_planes, x_offsets, x_gain, 3, 0, QUARTER, QUARTER)
+        gather(x_picked, x_planes, x_offsets, x_gain, 2, 1)
+        gather(x_picked, x_planes, x_offsets, x_gain, 3, 1)
+        x_woven = [keep.tile([P, PACK * QUARTER], BF16, name=f"x_woven{q}", align_bytes=64)[:] for q in range(4)]
+        for q in range(4):
+            interleave(x_woven[q], x_picked[q // 2], q % 2 * QUARTER)
 
         out_rows = out.rearrange("(n p) j -> p n j", p=P)
 
         def multiply_x(q):
-            codes, exps = quantize(x_woven[q], f"x{q}")
+            codes = keep.tile([P, QUARTER], U32, name=f"x_codes{q}", align_bytes=64)
+            exps = quantize(x_woven[q], codes[:], f"x_exp{q}")
             banks = []
             for pair in range(2):
                 bank = psum.tile([P, 2, QUARTER], F32, name="bank")
@@ -149,7 +195,8 @@ def tile_list_max_none_kernel(
 
         def finish(q, pair, bank):
             result = keep.tile([P, 2, QUARTER], F32, name=f"result{q}_{pair}")
-            nc.vector.tensor_tensor(result[:], bank[:], yb[q][:, 2 * pair : 2 * pair + 2, :], MAX)
+            j0 = q % 2 * QUARTER
+            nc.vector.tensor_tensor(result[:], bank[:], yb[q // 2][:, 2 * pair : 2 * pair + 2, j0 : j0 + QUARTER], MAX)
             nc.sync.dma_start(out_rows[:, 2 * pair : 2 * pair + 2, q * QUARTER : (q + 1) * QUARTER], result[:])
 
         banks = multiply_x(0)

@@ -125,8 +125,8 @@ def tile_list_max_none_kernel(
             width = woven.shape[1] // PACK
             planes = picked[:, : PACK * HALF].rearrange("p (i j) -> p i j", i=PACK)
             nc.scalar.copy(
-                woven.rearrange("p (c e i) -> p c i e", e=4, i=PACK),
-                planes[:, :, j0 : j0 + width].rearrange("p i (c e) -> p c i e", e=4),
+                woven.rearrange("p (c e i) -> p c i e", e=2, i=PACK),
+                planes[:, :, j0 : j0 + width].rearrange("p i (c e) -> p c i e", e=2),
             )
 
         def quantize(woven, codes, name):
@@ -193,15 +193,19 @@ def tile_list_max_none_kernel(
                 banks.append(bank)
             return banks
 
-        def finish(q, pair, bank):
-            result = keep.tile([P, 2, QUARTER], F32, name=f"result{q}_{pair}")
+        def finish(q, banks, n, count):
+            result = keep.tile([P, count, QUARTER], F32, name=f"result{q}_{n}")
             j0 = q % 2 * QUARTER
-            nc.vector.tensor_tensor(result[:], bank[:], yb[q // 2][:, 2 * pair : 2 * pair + 2, j0 : j0 + QUARTER], MAX)
-            nc.sync.dma_start(out_rows[:, 2 * pair : 2 * pair + 2, q * QUARTER : (q + 1) * QUARTER], result[:])
+            ya = banks[n // 2][:, n % 2 : n % 2 + count, :]
+            nc.vector.tensor_tensor(result[:], ya, yb[q // 2][:, n : n + count, j0 : j0 + QUARTER], MAX)
+            nc.sync.dma_start(out_rows[:, n : n + count, q * QUARTER : (q + 1) * QUARTER], result[:])
 
         banks = multiply_x(0)
-        for q in range(4):
-            finish(q, 0, banks[0])
-            following = multiply_x(q + 1) if q + 1 < 4 else None
-            finish(q, 1, banks[1])
+        for q in range(3):
+            finish(q, banks, 0, 2)
+            following = multiply_x(q + 1)
+            finish(q, banks, 2, 2)
             banks = following
+        finish(3, banks, 0, 2)
+        finish(3, banks, 2, 1)
+        finish(3, banks, 3, 1)

@@ -19,14 +19,18 @@ MAX = mybir.AluOpType.max
 
 P = 128
 PACK = 4
-GROUPS = 8
-GROUP_ROWS = P // GROUPS
-CHUNKS = J // P
-REPEAT = 8
+QUADRANT = 32
+QUADRANTS = P // QUADRANT
+SCALE_ROWS = 4
+LIST_ROWS = 16
 N_TILES = N // P
-BANK = 512
-HALF = 512
-QUARTER = 256
+PSUM_BANKS = 8
+HALF = J // 2
+QUARTER = J // 4
+REPEAT = 8
+CHUNKS = J // P
+CHUNKS_PER_HALF = HALF // P
+PAIR = 2
 
 
 def tile_list_max_none_kernel(
@@ -35,19 +39,16 @@ def tile_list_max_none_kernel(
     nc = tc.nc
     with ExitStack() as ctx:
         keep = ctx.enter_context(tc.tile_pool(name="keep", bufs=1))
-        psum = ctx.enter_context(tc.psum_pool(name="psum", bufs=8))
+        psum = ctx.enter_context(tc.psum_pool(name="psum", bufs=PSUM_BANKS))
 
-        z_offsets = keep.tile([P, J // 16], U16, name="z_offsets")
-        x_offsets = keep.tile([P, J // 16], U16, name="x_offsets")
+        z_offsets = keep.tile([P, J // LIST_ROWS], U16, name="z_offsets")
+        x_offsets = keep.tile([P, J // LIST_ROWS], U16, name="x_offsets")
         z_planes = [keep.tile([P, T], F32, name=f"z_plane{i}") for i in range(PACK)]
         x_planes = [keep.tile([P, T], F32, name=f"x_plane{i}", align_bytes=64) for i in range(PACK)]
-        z_picked = [keep.tile([P, PACK * HALF], F32, name=f"z_picked{h}") for h in range(2)]
-        x_picked = [
-            keep.tile([P, PACK * HALF], F32, name=f"x_picked{h}", align_bytes=64) for h in range(2)
-        ]
-        z_gain = [keep.tile([P, HALF], F32, name=f"z_gain{h}", align_bytes=64)[:] for h in range(2)]
-        x_gain1 = keep.tile([P, HALF], F32, name="x_gain1")
-        x_gain = [x_picked[1][:, 2 * HALF + QUARTER : 3 * HALF + QUARTER], x_gain1[:]]
+        z_picked = keep.tile([P, PACK * J], F32, name="z_picked")
+        x_picked = keep.tile([P, PACK * J], F32, name="x_picked")
+        z_gain = keep.tile([P, J], F32, name="z_gain", align_bytes=64)[:]
+        x_gain = keep.tile([P, J], F32, name="x_gain")[:]
         wa_codes = keep.tile([P, PACK * N], U8, name="wa_codes", align_bytes=64)
         wb_codes = keep.tile([P, 2 * N], U8, name="wb_codes", align_bytes=64)
         wa_exp = keep.tile([P, N], U8, name="wa_exp", align_bytes=64)
@@ -66,10 +67,11 @@ def tile_list_max_none_kernel(
         def load_compact(compact, gains):
             nc.sync.dma_start(compact[:], gains[0:P:REPEAT, :].rearrange("m (c j) -> m c j", j=P))
 
-        def load_scales(plane, scales):
-            for q in range(4):
+        def load_scales(exp_tile, scales):
+            for q in range(QUADRANTS):
                 nc.sync.dma_start(
-                    plane[32 * q : 32 * q + 4, :].bitcast(I32), scales[0, 4 * q : 4 * q + 4, :].bitcast(I32)
+                    exp_tile[QUADRANT * q : QUADRANT * q + SCALE_ROWS, :].bitcast(I32),
+                    scales[0, SCALE_ROWS * q : SCALE_ROWS * (q + 1), :].bitcast(I32),
                 )
 
         load_compact(z_compact, wgt2)
@@ -87,46 +89,45 @@ def tile_list_max_none_kernel(
             nc.sync.dma_start(x_planes[i][:], x_rows[i])
         nc.sync.dma_start(wa_codes[:].bitcast(I32), wa_words[0].rearrange("p n i -> p (n i)").bitcast(I32))
 
-        chunks = HALF // P
         z_turned = keep.tile([P, P], F32, name="z_turned", align_bytes=64)
         nc.vector.transpose(z_turned[:], z_compact[:])
         z_repeated = [keep.tile([P, HALF], F32, name=f"z_repeated{h}", align_bytes=64) for h in range(2)]
+        blocks, rows = P // QUADRANT, QUADRANT // REPEAT
         for h in range(2):
-            source = z_turned[:].rearrange("p (b m c) -> p c b m", b=4, m=4)[:, h * chunks : (h + 1) * chunks]
+            source = z_turned[:].rearrange("p (b m c) -> p c b m", b=blocks, m=rows)
+            source = source[:, h * CHUNKS_PER_HALF : (h + 1) * CHUNKS_PER_HALF]
             nc.vector.tensor_copy(
-                z_repeated[h][:].rearrange("p (c b m r) -> p c b m r", b=4, m=4, r=REPEAT),
-                source.unsqueeze(4).to_broadcast([P, chunks, 4, 4, REPEAT]),
+                z_repeated[h][:].rearrange("p (c b m r) -> p c b m r", b=blocks, m=rows, r=REPEAT),
+                source.unsqueeze(4).to_broadcast([P, CHUNKS_PER_HALF, blocks, rows, REPEAT]),
             )
         for h in range(2):
-            nc.vector.transpose(z_gain[h], z_repeated[h][:])
+            nc.vector.transpose(z_gain[:, h * HALF : (h + 1) * HALF], z_repeated[h][:])
 
         x_turned = psum.tile([P, P], F32, name="bank")
         nc.tensor.transpose(x_turned[:], x_compact[:], identity[:])
         for h in range(2):
-            source = x_turned[:].rearrange("p (m c) -> p c m", c=CHUNKS)[:, h * chunks : (h + 1) * chunks]
-            repeated = keep.tile([P, HALF], F32, name=f"x_repeated{h}")
+            source = x_turned[:].rearrange("p (m c) -> p c m", c=CHUNKS)
+            source = source[:, h * CHUNKS_PER_HALF : (h + 1) * CHUNKS_PER_HALF]
+            x_repeated = keep.tile([P, HALF], F32, name=f"x_repeated{h}")
             nc.scalar.copy(
-                repeated[:].rearrange("p (c m r) -> p c m r", c=chunks, r=REPEAT),
-                source.unsqueeze(3).to_broadcast([P, chunks, P // REPEAT, REPEAT]),
+                x_repeated[:].rearrange("p (c m r) -> p c m r", c=CHUNKS_PER_HALF, r=REPEAT),
+                source.unsqueeze(3).to_broadcast([P, CHUNKS_PER_HALF, P // REPEAT, REPEAT]),
             )
-            bank = psum.tile([P, BANK], F32, name="bank")
-            for c in range(chunks):
-                nc.tensor.transpose(bank[:, c * P : (c + 1) * P], repeated[:, c * P : (c + 1) * P], identity[:])
-            nc.scalar.copy(x_gain[h], bank[:])
+            bank = psum.tile([P, HALF], F32, name="bank")
+            for c in range(CHUNKS_PER_HALF):
+                nc.tensor.transpose(bank[:, c * P : (c + 1) * P], x_repeated[:, c * P : (c + 1) * P], identity[:])
+            nc.scalar.copy(x_gain[:, h * HALF : (h + 1) * HALF], bank[:])
 
-        def gather(picked, planes, offsets, gain, i, h, j0=0, width=HALF):
-            first = h * HALF + j0
-            window = planes[i][:].indirect(offsets[:, first // 16 : (first + width) // 16])
-            nc.vector.tensor_tensor(
-                picked[h][:, i * HALF + j0 : i * HALF + j0 + width], window, gain[h][:, j0 : j0 + width], MULT
-            )
+        def gather(picked, planes, offsets, gain, i, j0, width):
+            window = planes[i][:].indirect(offsets[:, j0 // LIST_ROWS : (j0 + width) // LIST_ROWS])
+            nc.vector.tensor_tensor(picked[:, i * J + j0 : i * J + j0 + width], window, gain[:, j0 : j0 + width], MULT)
 
         def interleave(woven, picked, j0):
             width = woven.shape[1] // PACK
-            planes = picked[:, : PACK * HALF].rearrange("p (i j) -> p i j", i=PACK)
+            by_plane = picked[:].rearrange("p (i j) -> p i j", i=PACK)
             nc.scalar.copy(
-                woven.rearrange("p (c e i) -> p c i e", e=2, i=PACK),
-                planes[:, :, j0 : j0 + width].rearrange("p i (c e) -> p c i e", e=2),
+                woven.rearrange("p (c e i) -> p c i e", e=PAIR, i=PACK),
+                by_plane[:, :, j0 : j0 + width].rearrange("p i (c e) -> p c i e", e=PAIR),
             )
 
         def quantize(woven, codes, name):
@@ -134,22 +135,22 @@ def tile_list_max_none_kernel(
             nc.vector.quantize_mx(out=codes.bitcast(FP8X4), scales=exps[:], in_=woven)
             return exps
 
-        for i in range(PACK):
-            for h in range(2):
-                gather(z_picked, z_planes, z_offsets, z_gain, i, h)
+        for i in range(PACK - 1):
+            gather(z_picked, z_planes, z_offsets, z_gain, i, 0, J)
+        for h in range(2):
+            gather(z_picked, z_planes, z_offsets, z_gain, PACK - 1, h * HALF, HALF)
         z_woven = [keep.tile([P, PACK * HALF], BF16, name=f"z_woven{h}", align_bytes=64)[:] for h in range(2)]
         for h in range(2):
-            interleave(z_woven[h], z_picked[h], 0)
+            interleave(z_woven[h], z_picked, h * HALF)
 
         yb = [keep.tile([P, N_TILES, HALF], F32, name=f"yb{h}") for h in range(2)]
-        for h in range(2):
-            gather(x_picked, x_planes, x_offsets, x_gain, 0, h)
+        gather(x_picked, x_planes, x_offsets, x_gain, 0, 0, J)
         z_codes = keep.tile([P, J], U32, name="z_codes", tag="x_plane0", align_bytes=64)
         for h in range(2):
             codes = z_codes[:, h * HALF : (h + 1) * HALF]
             exps = quantize(z_woven[h], codes, f"z_exp{h}")
             for n in range(N_TILES):
-                bank = psum.tile([P, BANK], F32, name="bank")
+                bank = psum.tile([P, HALF], F32, name="bank")
                 nc.tensor.matmul_mx(
                     out=bank[:],
                     lhsT=wb_codes[:, 2 * P * n : 2 * P * (n + 1)].bitcast(FP4X4),
@@ -160,29 +161,27 @@ def tile_list_max_none_kernel(
                     stop=True,
                 )
                 nc.scalar.copy(yb[h][:, n, :], bank[:])
-        for h in range(2):
-            gather(x_picked, x_planes, x_offsets, x_gain, 1, h)
-        gather(x_picked, x_planes, x_offsets, x_gain, 2, 0)
-        gather(x_picked, x_planes, x_offsets, x_gain, 3, 0, 0, QUARTER)
-        gather(x_picked, x_planes, x_offsets, x_gain, 3, 0, QUARTER, QUARTER)
-        gather(x_picked, x_planes, x_offsets, x_gain, 2, 1)
-        gather(x_picked, x_planes, x_offsets, x_gain, 3, 1)
+
+        for i in range(1, PACK - 1):
+            gather(x_picked, x_planes, x_offsets, x_gain, i, 0, J)
+        for j0, width in ((0, QUARTER), (QUARTER, QUARTER), (HALF, HALF)):
+            gather(x_picked, x_planes, x_offsets, x_gain, PACK - 1, j0, width)
         x_woven = [keep.tile([P, PACK * QUARTER], BF16, name=f"x_woven{q}", align_bytes=64)[:] for q in range(4)]
         for q in range(4):
-            interleave(x_woven[q], x_picked[q // 2], q % 2 * QUARTER)
+            interleave(x_woven[q], x_picked, q * QUARTER)
 
         out_rows = out.rearrange("(n p) j -> p n j", p=P)
 
         def multiply_x(q):
             codes = keep.tile([P, QUARTER], U32, name=f"x_codes{q}", align_bytes=64)
             exps = quantize(x_woven[q], codes[:], f"x_exp{q}")
-            banks = []
-            for pair in range(2):
-                bank = psum.tile([P, 2, QUARTER], F32, name="bank")
+            ya_banks = []
+            for first in range(0, N_TILES, 2):
+                ya_bank = psum.tile([P, 2, QUARTER], F32, name="bank")
                 for u in range(2):
-                    n = 2 * pair + u
+                    n = first + u
                     nc.tensor.matmul_mx(
-                        out=bank[:, u, :],
+                        out=ya_bank[:, u, :],
                         lhsT=wa_codes[:, PACK * P * n : PACK * P * (n + 1)].bitcast(FP8X4),
                         lhsT_scale=wa_exp[:, P * n : P * (n + 1)],
                         rhs=codes[:].bitcast(FP8X4),
@@ -190,13 +189,13 @@ def tile_list_max_none_kernel(
                         start=True,
                         stop=True,
                     )
-                banks.append(bank)
-            return banks
+                ya_banks.append(ya_bank)
+            return ya_banks
 
-        def finish(q, banks, n, count):
+        def finish(q, ya_banks, n, count):
             result = keep.tile([P, count, QUARTER], F32, name=f"result{q}_{n}")
             j0 = q % 2 * QUARTER
-            ya = banks[n // 2][:, n % 2 : n % 2 + count, :]
+            ya = ya_banks[n // 2][:, n % 2 : n % 2 + count, :]
             nc.vector.tensor_tensor(result[:], ya, yb[q // 2][:, n : n + count, j0 : j0 + QUARTER], MAX)
             nc.sync.dma_start(out_rows[:, n : n + count, q * QUARTER : (q + 1) * QUARTER], result[:])
 

from contextlib import ExitStack

import concourse.mybir as mybir
from concourse.masks import make_identity

K, N, T, J = 512, 512, 2048, 1024
FLOPS = 2 * 2 * K * N * J

F32 = mybir.dt.float32
BF16 = mybir.dt.bfloat16
I32 = mybir.dt.int32
U32 = mybir.dt.uint32
U16 = mybir.dt.uint16
U8 = mybir.dt.uint8
FP8X4 = mybir.dt.float8_e4m3fn_x4
FP4X4 = mybir.dt.float4_e2m1fn_x4
MULT = mybir.AluOpType.mult
MAX = mybir.AluOpType.max

P = 128
PACK = 4
QUADRANT = 32
QUADRANTS = P // QUADRANT
SCALE_ROWS = 4
LIST_ROWS = 16
N_TILES = N // P
PSUM_BANKS = 8
HALF = J // 2
QUARTER = J // 4
REPEAT = 8
CHUNKS = J // P
CHUNKS_PER_HALF = HALF // P
PAIR = 2


def tile_list_max_none_kernel(
    tc, xT, wgt, zT, wgt2, wa_words, wa_scales, wb_words, wb_scales, offs, offs2, out
):
    nc = tc.nc
    with ExitStack() as ctx:
        keep = ctx.enter_context(tc.tile_pool(name="keep", bufs=1))
        psum = ctx.enter_context(tc.psum_pool(name="psum", bufs=PSUM_BANKS))

        z_offsets = keep.tile([P, J // LIST_ROWS], U16, name="z_offsets")
        x_offsets = keep.tile([P, J // LIST_ROWS], U16, name="x_offsets")
        z_planes = [keep.tile([P, T], F32, name=f"z_plane{i}") for i in range(PACK)]
        x_planes = [keep.tile([P, T], F32, name=f"x_plane{i}", align_bytes=64) for i in range(PACK)]
        z_picked = keep.tile([P, PACK * J], F32, name="z_picked")
        x_picked = keep.tile([P, PACK * J], F32, name="x_picked")
        z_gain = keep.tile([P, J], F32, name="z_gain", align_bytes=64)[:]
        x_gain = keep.tile([P, J], F32, name="x_gain")[:]
        wa_codes = keep.tile([P, PACK * N], U8, name="wa_codes", align_bytes=64)
        wb_codes = keep.tile([P, 2 * N], U8, name="wb_codes", align_bytes=64)
        wa_exp = keep.tile([P, N], U8, name="wa_exp", align_bytes=64)
        wb_exp = keep.tile([P, N], U8, name="wb_exp", align_bytes=64)
        z_compact = keep.tile([P, P], F32, name="z_compact", align_bytes=64)
        x_compact = keep.tile([P, P], F32, name="x_compact")
        identity = keep.tile([P, P], F32, name="identity")

        z_rows = zT.rearrange("(p i) t -> i p t", i=PACK)
        x_rows = xT.rearrange("(p i) t -> i p t", i=PACK)

        make_identity(nc, identity[:])
        nc.vector.memset(wb_exp[:].bitcast(I32), 0)
        nc.vector.memset(wa_exp[:].bitcast(I32), 0)

        def load_compact(compact, gains):
            nc.sync.dma_start(compact[:], gains[0:P:REPEAT, :].rearrange("m (c j) -> m c j", j=P))

        def load_scales(exp_tile, scales):
            for q in range(QUADRANTS):
                nc.sync.dma_start(
                    exp_tile[QUADRANT * q : QUADRANT * q + SCALE_ROWS, :].bitcast(I32),
                    scales[0, SCALE_ROWS * q : SCALE_ROWS * (q + 1), :].bitcast(I32),
                )

        load_compact(z_compact, wgt2)
        nc.sync.dma_start(z_offsets[:], offs2)
        nc.sync.dma_start(z_planes[0][:], z_rows[0])
        load_compact(x_compact, wgt)
        for i in range(1, PACK):
            nc.sync.dma_start(z_planes[i][:], z_rows[i])
        nc.sync.dma_start(x_offsets[:], offs)
        load_scales(wb_exp, wb_scales)
        nc.sync.dma_start(x_planes[0][:], x_rows[0])
        nc.sync.dma_start(wb_codes[:].bitcast(I32), wb_words[0].bitcast(I32))
        load_scales(wa_exp, wa_scales)
        for i in range(1, PACK):
            nc.sync.dma_start(x_planes[i][:], x_rows[i])
        nc.sync.dma_start(wa_codes[:].bitcast(I32), wa_words[0].rearrange("p n i -> p (n i)").bitcast(I32))

        z_turned = keep.tile([P, P], F32, name="z_turned", align_bytes=64)
        nc.vector.transpose(z_turned[:], z_compact[:])
        z_repeated = [keep.tile([P, HALF], F32, name=f"z_repeated{h}", align_bytes=64) for h in range(2)]
        blocks, rows = P // QUADRANT, QUADRANT // REPEAT
        for h in range(2):
            source = z_turned[:].rearrange("p (b m c) -> p c b m", b=blocks, m=rows)
            source = source[:, h * CHUNKS_PER_HALF : (h + 1) * CHUNKS_PER_HALF]
            nc.vector.tensor_copy(
                z_repeated[h][:].rearrange("p (c b m r) -> p c b m r", b=blocks, m=rows, r=REPEAT),
                source.unsqueeze(4).to_broadcast([P, CHUNKS_PER_HALF, blocks, rows, REPEAT]),
            )
        for h in range(2):
            nc.vector.transpose(z_gain[:, h * HALF : (h + 1) * HALF], z_repeated[h][:])

        x_turned = psum.tile([P, P], F32, name="bank")
        nc.tensor.transpose(x_turned[:], x_compact[:], identity[:])
        for h in range(2):
            source = x_turned[:].rearrange("p (m c) -> p c m", c=CHUNKS)
            source = source[:, h * CHUNKS_PER_HALF : (h + 1) * CHUNKS_PER_HALF]
            x_repeated = keep.tile([P, HALF], F32, name=f"x_repeated{h}")
            nc.scalar.copy(
                x_repeated[:].rearrange("p (c m r) -> p c m r", c=CHUNKS_PER_HALF, r=REPEAT),
                source.unsqueeze(3).to_broadcast([P, CHUNKS_PER_HALF, P // REPEAT, REPEAT]),
            )
            bank = psum.tile([P, HALF], F32, name="bank")
            for c in range(CHUNKS_PER_HALF):
                nc.tensor.transpose(bank[:, c * P : (c + 1) * P], x_repeated[:, c * P : (c + 1) * P], identity[:])
            nc.scalar.copy(x_gain[:, h * HALF : (h + 1) * HALF], bank[:])

        def gather(picked, planes, offsets, gain, i, j0, width):
            window = planes[i][:].indirect(offsets[:, j0 // LIST_ROWS : (j0 + width) // LIST_ROWS])
            nc.vector.tensor_tensor(picked[:, i * J + j0 : i * J + j0 + width], window, gain[:, j0 : j0 + width], MULT)

        def interleave(woven, picked, j0):
            width = woven.shape[1] // PACK
            by_plane = picked[:].rearrange("p (i j) -> p i j", i=PACK)
            nc.scalar.copy(
                woven.rearrange("p (c e i) -> p c i e", e=PAIR, i=PACK),
                by_plane[:, :, j0 : j0 + width].rearrange("p i (c e) -> p c i e", e=PAIR),
            )

        def quantize(woven, codes, name):
            exps = keep.tile([P, codes.shape[1]], U8, name=name, align_bytes=64)
            nc.vector.quantize_mx(out=codes.bitcast(FP8X4), scales=exps[:], in_=woven)
            return exps

        for i in range(PACK - 1):
            gather(z_picked, z_planes, z_offsets, z_gain, i, 0, J)
        for h in range(2):
            gather(z_picked, z_planes, z_offsets, z_gain, PACK - 1, h * HALF, HALF)
        z_woven = [keep.tile([P, PACK * HALF], BF16, name=f"z_woven{h}", align_bytes=64)[:] for h in range(2)]
        for h in range(2):
            interleave(z_woven[h], z_picked, h * HALF)

        yb = [keep.tile([P, N_TILES, HALF], F32, name=f"yb{h}") for h in range(2)]
        gather(x_picked, x_planes, x_offsets, x_gain, 0, 0, J)
        z_codes = keep.tile([P, J], U32, name="z_codes", tag="x_plane0", align_bytes=64)
        for h in range(2):
            codes = z_codes[:, h * HALF : (h + 1) * HALF]
            exps = quantize(z_woven[h], codes, f"z_exp{h}")
            for n in range(N_TILES):
                bank = psum.tile([P, HALF], F32, name="bank")
                nc.tensor.matmul_mx(
                    out=bank[:],
                    lhsT=wb_codes[:, 2 * P * n : 2 * P * (n + 1)].bitcast(FP4X4),
                    lhsT_scale=wb_exp[:, P * n : P * (n + 1)],
                    rhs=codes.bitcast(FP8X4),
                    rhs_scale=exps[:],
                    start=True,
                    stop=True,
                )
                nc.scalar.copy(yb[h][:, n, :], bank[:])

        for i in range(1, PACK - 1):
            gather(x_picked, x_planes, x_offsets, x_gain, i, 0, J)
        for j0, width in ((0, QUARTER), (QUARTER, QUARTER), (HALF, HALF)):
            gather(x_picked, x_planes, x_offsets, x_gain, PACK - 1, j0, width)
        x_woven = [keep.tile([P, PACK * QUARTER], BF16, name=f"x_woven{q}", align_bytes=64)[:] for q in range(4)]
        for q in range(4):
            interleave(x_woven[q], x_picked, q * QUARTER)

        out_rows = out.rearrange("(n p) j -> p n j", p=P)

        def multiply_x(q):
            codes = keep.tile([P, QUARTER], U32, name=f"x_codes{q}", align_bytes=64)
            exps = quantize(x_woven[q], codes[:], f"x_exp{q}")
            ya_banks = []
            for first in range(0, N_TILES, 2):
                ya_bank = psum.tile([P, 2, QUARTER], F32, name="bank")
                for u in range(2):
                    n = first + u
                    nc.tensor.matmul_mx(
                        out=ya_bank[:, u, :],
                        lhsT=wa_codes[:, PACK * P * n : PACK * P * (n + 1)].bitcast(FP8X4),
                        lhsT_scale=wa_exp[:, P * n : P * (n + 1)],
                        rhs=codes[:].bitcast(FP8X4),
                        rhs_scale=exps[:],
                        start=True,
                        stop=True,
                    )
                ya_banks.append(ya_bank)
            return ya_banks

        def finish(q, ya_banks, n, count):
            result = keep.tile([P, count, QUARTER], F32, name=f"result{q}_{n}")
            j0 = q % 2 * QUARTER
            ya = ya_banks[n // 2][:, n % 2 : n % 2 + count, :]
            nc.vector.tensor_tensor(result[:], ya, yb[q // 2][:, n : n + count, j0 : j0 + QUARTER], MAX)
            nc.sync.dma_start(out_rows[:, n : n + count, q * QUARTER : (q + 1) * QUARTER], result[:])

        banks = multiply_x(0)
        for q in range(3):
            finish(q, banks, 0, 2)
            following = multiply_x(q + 1)
            finish(q, banks, 2, 2)
            banks = following
        finish(3, banks, 0, 2)
        finish(3, banks, 2, 1)
        finish(3, banks, 3, 1)
